import numpy as np
import ml_dtypes


def mxq(x, axis, fmt="e4m3"):
    dtype, down = {"e4m3": (ml_dtypes.float8_e4m3fn, 7), "e5m2": (ml_dtypes.float8_e5m2, 14)}[fmt]
    v = np.moveaxis(np.asarray(x, np.float32).astype(ml_dtypes.bfloat16).astype(np.float64), axis, -1)
    blocks = v.reshape(v.shape[:-1] + (-1, 32))
    amax = np.abs(blocks).max(-1, keepdims=True)
    byte = np.maximum(np.where(amax > 0, np.frexp(amax)[1] - 1 + 127, 0) - down, 1)
    scale = np.exp2(byte - 127.0)
    codes = (blocks / scale).astype(np.float32).astype(dtype).astype(np.float64)
    return np.moveaxis((codes * scale).reshape(v.shape), -1, axis)


WIDE = False


def mx_kscale(k):
    if not WIDE:
        return np.ones(k)
    levels = np.array([10, -10, 5, -5, 0])
    if k % 512:
        return np.exp2(np.random.permutation(np.resize(levels, k // 32))).repeat(32)
    a = np.empty((k // 512, 16))
    for p in range(k // 512):
        a[p, :8] = np.random.permutation(np.resize(levels, 8))
        for g in range(8):
            far = levels[np.abs(levels - a[p, g]) >= 10]
            a[p, g + 8] = far[np.random.randint(len(far))]
    return np.exp2(a.ravel()).repeat(32)


def f64(x):
    return np.asarray(x).astype(np.float64)


def striped(idx):
    return np.tile(idx.reshape(-1, 16).T, (8, 1)).astype(np.uint16)


def unstriped(offs):
    return offs[:16].T.reshape(-1).astype(np.int64)


def pack_weight(w):
    k, n = w.shape
    w = f64(np.asarray(w, np.float32).astype(ml_dtypes.bfloat16)).reshape(k // 32, 32, n)
    amax = np.abs(w).max(1)
    byte = np.clip(np.where(amax > 0, np.frexp(amax)[1] - 1 + 127 - 7, 1), 1, 254)
    scaled = (w * np.exp2(127.0 - byte)[:, None, :]).reshape(k, n).astype(np.float32)
    words = np.ascontiguousarray(scaled.reshape(k // 512, 128, 4, n).transpose(0, 1, 3, 2)).astype(ml_dtypes.float8_e4m3fn).view(np.uint8)
    return words, np.ascontiguousarray(byte.astype(np.uint8).reshape(k // 512, 16, n))


def unpack_weight(words, scales):
    g, p, n, _ = words.shape
    vals = np.ascontiguousarray(words).view(ml_dtypes.float8_e4m3fn).astype(np.float64) * np.repeat(np.exp2(scales.astype(np.float64) - 127.0), 8, axis=1)[..., None]
    return vals.transpose(0, 1, 3, 2).reshape(g * 512, n)


E2M1 = np.array([0.0, 0.5, 1.0, 1.5, 2.0, 3.0, 4.0, 6.0, -0.0, -0.5, -1.0, -1.5, -2.0, -3.0, -4.0, -6.0])


def pack_fp4(w):
    k, n = w.shape
    w = f64(np.asarray(w, np.float32).astype(ml_dtypes.bfloat16)).reshape(k // 32, 32, n)
    amax = np.abs(w).max(1)
    mant, ex = np.frexp(amax / 6.0)
    byte = np.clip(np.where(amax > 0, np.where(mant > 0.5, ex, ex - 1) + 127, 1), 1, 254)
    scaled = (w * np.exp2(127.0 - byte)[:, None, :]).reshape(k, n).astype(np.float32)
    c = np.ascontiguousarray(scaled.reshape(k // 512, 128, 4, n).transpose(0, 1, 3, 2)).astype(ml_dtypes.float4_e2m1fn).view(np.uint8) & 0xF
    words = (c[..., 0::2] | (c[..., 1::2] << 4)).reshape(k // 512, 128, 2 * n)
    return np.ascontiguousarray(words), np.ascontiguousarray(byte.astype(np.uint8).reshape(k // 512, 16, n))


def unpack_fp4(words, scales):
    g, _, n = scales.shape
    words = np.ascontiguousarray(words).reshape(g, 128, n, 2)
    nib = np.empty((g, 128, n, 4), np.uint8)
    nib[..., 0::2] = words & 0xF
    nib[..., 1::2] = words >> 4
    vals = E2M1[nib] * np.repeat(np.exp2(scales.astype(np.float64) - 127.0), 8, axis=1)[..., None]
    return vals.transpose(0, 1, 3, 2).reshape(g * 512, n)


K, T, S, N, H = 1024, 2048, 512, 256, 512


def setup_inputs():
    n = np.random.standard_normal
    s = mx_kscale(K)[:, None]
    u = mx_kscale(H)
    packed_xT = pack_weight(n((K, T)) * s)
    packed_w1 = pack_fp4(n((K, H)) / np.sqrt(K) / s)
    packed_w2 = pack_fp4(n((K, H)) / np.sqrt(K) / s)
    packed_w3 = pack_fp4(n((H, N)) / np.sqrt(H) / u[:, None])
    return {
        "x_words": packed_xT[0],
        "x_scales": packed_xT[1],
        "w1_words": packed_w1[0],
        "w1_scales": packed_w1[1],
        "w2_words": packed_w2[0],
        "w2_scales": packed_w2[1],
        "kpin": (np.random.uniform(0.2, 0.6, (H, 1))).astype(np.float32),
        "unit": (np.random.uniform(0.6, 1.4, (H, 1)) * u[:, None]).astype(np.float32),
        "w3_words": packed_w3[0],
        "w3_scales": packed_w3[1],
        "offs": striped(np.random.permutation(T)[:S]),
        "nn1": striped(np.random.permutation(S)),
        "nn2": striped(np.random.permutation(S)),
    }


def reference(x_words, x_scales, w1_words, w1_scales, w2_words, w2_scales, kpin, unit, w3_words, w3_scales, offs, nn1, nn2):
    xq = unpack_weight(x_words, x_scales)[:, unstriped(offs)]
    mg = unpack_fp4(w2_words, w2_scales).T @ xq
    mag = np.tanh(mg)
    hf = unpack_fp4(w1_words, w1_scales).T @ xq
    m1 = mag[:, unstriped(nn1)]
    m2 = mag[:, unstriped(nn2)]
    heff = hf + 0.6 * mag + 0.3 * (m1 + m2)
    anh = heff / (np.abs(heff) + 0.8)
    pin = (anh - mag) / (np.abs(anh - mag) + 0.4)
    irr = mag + f64(kpin) * pin
    loss = irr - mag
    hid = f64(unit) * (loss * heff)
    return unpack_fp4(w3_words, w3_scales).T @ mxq(hid, 0, "e4m3")

@@ -1,0 +1,242 @@
+from contextlib import ExitStack
+
+import concourse.mybir as mybir
+from concourse.masks import make_identity
+
+K, T, S, N, H = 1024, 2048, 512, 256, 512
+FLOPS = 2 * (2 * K * H * S + H * N * S)
+
+F32 = mybir.dt.float32
+BF16 = mybir.dt.bfloat16
+I32 = mybir.dt.int32
+U32 = mybir.dt.uint32
+U16 = mybir.dt.uint16
+U8 = mybir.dt.uint8
+FP8X4 = mybir.dt.float8_e4m3fn_x4
+FP4X4 = mybir.dt.float4_e2m1fn_x4
+ALU = mybir.AluOpType
+ACT = mybir.ActivationFunctionType
+
+P = 128
+PACK = 4
+PASSES = K // (P * PACK)
+SPARE = 8
+BLOCKS = S // P
+
+
+def tile_picked_yhystr_loss_p_kernel(
+    tc, x_words, x_scales, w1_words, w1_scales, w2_words, w2_scales, kpin, unit, w3_words, w3_scales, offs, nn1, nn2, out
+):
+    nc = tc.nc
+    with ExitStack() as ctx:
+        keep = ctx.enter_context(tc.tile_pool(name="keep", bufs=1))
+        ring = ctx.enter_context(tc.tile_pool(name="ring", bufs=2))
+        psum = ctx.enter_context(tc.psum_pool(name="psum", bufs=1))
+        psum2 = ctx.enter_context(tc.psum_pool(name="psum2", bufs=2))
+
+        def load_list(name, src):
+            tile = keep.tile([P, S // 16], U16, name=name)
+            nc.sync.dma_start(tile[:], src)
+            return tile
+
+        def clear_plane(name, src, engine):
+            passes, rows, width = src.shape
+            plane = keep.tile([P, passes * width], U8, name=name, align_bytes=64)
+            engine.memset(plane[:].bitcast(I32), 0)
+            return plane
+
+        def load_scales(plane, src, queue):
+            for q in range(4):
+                queue.dma_start(
+                    plane[32 * q : 32 * q + 4, : src.shape[0] * src.shape[2]].bitcast(I32).rearrange("r (o c) -> r o c", o=src.shape[0]),
+                    src[:, 4 * q : 4 * q + 4, :].bitcast(I32).rearrange("o r c -> r o c"),
+                )
+
+        def load_words(name, src):
+            passes, rows, width = src.shape
+            words = keep.tile([P, passes * width], U8, name=name, align_bytes=64)
+            nc.sync.dma_start(
+                words[:].bitcast(I32).rearrange("p (o c) -> p o c", o=passes),
+                src.bitcast(I32).rearrange("o p c -> p o c"),
+            )
+            return words
+
+        def load_table(o):
+            table = keep.tile([P, T], U32, name="x_table%d" % o, tag="table%d" % o, align_bytes=64)
+            nc.sync.dma_start(table[:].bitcast(I32), x_words[o].rearrange("p c r -> p (c r)").bitcast(I32))
+            return table
+
+        def deal_words(name, words):
+            dealt = keep.tile([P, PASSES * H * 2], U8, name=name, align_bytes=64)
+            nc.scalar.copy(
+                dealt[:].bitcast(U16).rearrange("p (o t m) -> p o t m", o=PASSES, t=PACK),
+                words[:].bitcast(U16).rearrange("p (o m t) -> p o t m", o=PASSES, t=PACK),
+            )
+            return dealt
+
+        def deal_scales(dealt, plane):
+            nc.vector.tensor_copy(
+                dealt[:].rearrange("p (o t m) -> p o t m", o=PASSES, t=PACK),
+                plane[:].rearrange("p (o m t) -> p o t m", o=PASSES, t=PACK),
+            )
+
+        w2_plane = clear_plane("w2_plane", w2_scales, nc.gpsimd)
+        x_plane = clear_plane("x_plane", x_scales, nc.vector)
+        w1_plane = clear_plane("w1_plane", w1_scales, nc.vector)
+        w3_plane = clear_plane("w3_plane", w3_scales, nc.vector)
+        picks = load_list("picks", offs)
+        w2_raw = load_words("w2_raw", w2_words)
+        first = load_list("first", nn1)
+        second = load_list("second", nn2)
+        load_scales(x_plane, x_scales, nc.sync)
+        load_scales(w2_plane, w2_scales, nc.gpsimd)
+        load_scales(w1_plane, w1_scales, nc.gpsimd)
+        x_table = [load_table(o) for o in range(PASSES)]
+        w1_raw = load_words("w1_raw", w1_words)
+        kpin_sb = keep.tile([P, PACK], F32)
+        unit_sb = keep.tile([P, PACK], F32)
+        nc.sync.dma_start(kpin_sb[:], kpin.rearrange("(p t) o -> p (t o)", t=PACK))
+        nc.sync.dma_start(unit_sb[:], unit.rearrange("(p t) o -> p (t o)", t=PACK))
+        w3_sb = load_words("w3_sb", w3_words)
+        load_scales(w3_plane, w3_scales, nc.sync)
+
+        ident = keep.tile([P, P], F32)
+        make_identity(nc, ident[:])
+        mag = [keep.tile([P, S + SPARE], F32, name="mag%d" % t) for t in range(PACK)]
+        for t in range(PACK):
+            nc.gpsimd.memset(mag[t][:, S:], 0.0)
+
+        x_bytes = [keep.tile([P, S], U8, name="x_bytes%d" % o, align_bytes=64) for o in range(PASSES)]
+        x_codes = [keep.tile([P, S], U32, name="x_codes%d" % o, align_bytes=64) for o in range(PASSES)]
+        w2_codes = deal_words("w2_codes", w2_raw)
+        w2_bytes = keep.tile([P, PASSES * H], U8, align_bytes=64)
+        for o in range(PASSES):
+            nc.vector.tensor_copy(x_bytes[o][:], x_plane[:, o * T : (o + 1) * T].indirect(picks[:]))
+        deal_scales(w2_bytes, w2_plane)
+        for o in range(PASSES):
+            nc.vector.tensor_copy(x_codes[o][:], x_table[o][:].indirect(picks[:]))
+        w1_codes = deal_words("w1_codes", w1_raw)
+        w1_bytes = keep.tile([P, PASSES * H], U8, tag="table1", align_bytes=64)
+        deal_scales(w1_bytes, w1_plane)
+        gain = keep.tile([P, PACK], F32)
+        nc.gpsimd.tensor_tensor(gain[:], kpin_sb[:], unit_sb[:], ALU.mult)
+
+        def first_pass(acc, codes, scale_bytes, t, o):
+            col = (o * PACK + t) * P
+            nc.tensor.matmul_mx(
+                out=acc[:],
+                lhsT=codes[:, 2 * col : 2 * (col + P)].bitcast(FP4X4),
+                lhsT_scale=scale_bytes[:, col : col + P],
+                rhs=x_codes[o][:].bitcast(FP8X4),
+                rhs_scale=x_bytes[o][:],
+                start=(o == 0),
+                stop=(o == PASSES - 1),
+            )
+
+        mg = [psum.tile([P, S], F32, name="mg%d" % t, tag="bank%d" % t) for t in range(PACK)]
+
+        def magnetise(t):
+            for o in range(PASSES):
+                first_pass(mg[t], w2_codes, w2_bytes, t, o)
+            nc.scalar.activation(mag[t][:, :S], mg[t][:], ACT.Tanh)
+
+        heff = keep.tile([P, PACK, S], F32)
+        absh = keep.tile([P, PACK, S], F32)
+        num = keep.tile([P, PACK, S], F32)
+        prod = keep.tile([P, PACK, S], F32)
+
+        def field(t):
+            m1 = ring.tile([P, S], F32, name="m1")
+            nc.scalar.activation(m1[:], mag[t][:].indirect(first[:]), ACT.Copy)
+            if t + 1 < PACK:
+                magnetise(t + 1)
+            hf = psum2.tile([P, S], F32, name="hf", tag="acc")
+            for o in range(PASSES):
+                first_pass(hf, w1_codes, w1_bytes, t, o)
+            both = keep.tile([P, S], F32, name="both")
+            if t == 0:
+                m2 = keep.tile([P, S], F32)
+                for half in range(2):
+                    nc.vector.tensor_copy(
+                        m2[:, half * S // 2 : (half + 1) * S // 2],
+                        mag[t][:].indirect(second[:, half * S // 32 : (half + 1) * S // 32]),
+                    )
+                nc.vector.tensor_tensor(both[:], m2[:], m1[:], ALU.add)
+            else:
+                nc.vector.tensor_tensor(both[:], mag[t][:].indirect(second[:]), m1[:], ALU.add)
+            own = ring.tile([P, S], F32, name="own")
+            nc.vector.scalar_tensor_tensor(own[:], mag[t][:, :S], 0.6, hf[:], ALU.mult, ALU.add)
+            nc.vector.scalar_tensor_tensor(heff[:, t, :], both[:], 0.3, own[:], ALU.mult, ALU.add)
+            nc.scalar.activation(absh[:, t, :], heff[:, t, :], ACT.Abs, scale=0.4)
+
+        def numerator(t, lo, hi):
+            pull = ring.tile([P, hi - lo], F32, name="pull")
+            nc.vector.scalar_tensor_tensor(pull[:], absh[:, t, lo:hi], 0.32, mag[t][:, lo:hi], ALU.add, ALU.mult)
+            nc.vector.scalar_tensor_tensor(num[:, t, lo:hi], pull[:], -2.5, heff[:, t, lo:hi], ALU.mult, ALU.add)
+
+        def inverse(t, lo, hi):
+            width = hi - lo
+            absn = ring.tile([P, width], F32, name="absn")
+            nc.scalar.activation(absn[:], num[:, t, lo:hi], ACT.Abs)
+            den = psum2.tile([P, width], F32, name="den", tag="den")
+            for c in range(0, width, P):
+                nc.tensor.matmul(den[:, c : c + P], absh[:, t, lo + c : lo + c + P], ident[:], start=True, stop=False, is_transpose=True)
+                nc.tensor.matmul(den[:, c : c + P], absn[:, c : c + P], ident[:], start=False, stop=True, is_transpose=True)
+            root = ring.tile([P, width], F32, name="root")
+            nc.scalar.activation(root[:], den[:], ACT.Abs_reciprocal_sqrt, bias=0.32)
+            turned = ring.tile([P, width], F32, name="turned")
+            nc.scalar.activation(turned[:], root[:], ACT.Square)
+            for c in range(0, width, P):
+                nc.tensor.transpose(inv[(lo + c) // P][:, t, :], turned[:, c : c + P], ident[:])
+
+        def product(t):
+            nc.vector.scalar_tensor_tensor(prod[:, t, :], heff[:, t, :], gain[:, t : t + 1], num[:, t, :], ALU.mult, ALU.mult)
+
+        def coils(b):
+            cols = slice(b * P, (b + 1) * P)
+            hid = ring.tile([P, P * PACK], BF16, name="hid", align_bytes=64)
+            nc.vector.tensor_tensor(
+                hid[:].rearrange("p (c i t) -> p c t i", i=4, t=PACK),
+                prod[:, :, cols].rearrange("p t (c i) -> p c t i", i=4),
+                inv[b][:].rearrange("p t (c i) -> p c t i", i=4),
+                ALU.mult,
+            )
+            codes = ring.tile([P, P], U32, name="codes", align_bytes=64)
+            scale_bytes = ring.tile([P, P], U8, name="scale_bytes", align_bytes=64)
+            nc.vector.quantize_mx(out=codes[:].bitcast(FP8X4), scales=scale_bytes[:], in_=hid[:])
+            acc = psum2.tile([P, N // P, P], F32, name="acc", tag="acc")
+            for a in range(N // P):
+                nc.tensor.matmul_mx(
+                    out=acc[:, a, :],
+                    lhsT=w3_sb[:, 2 * a * P : 2 * (a + 1) * P].bitcast(FP4X4),
+                    lhsT_scale=w3_plane[:, a * P : (a + 1) * P],
+                    rhs=codes[:].bitcast(FP8X4),
+                    rhs_scale=scale_bytes[:],
+                    start=True,
+                    stop=True,
+                )
+            res = keep.tile([P, N // P, P], F32, name="res%d" % b)
+            nc.scalar.copy(res[:], acc[:])
+            nc.sync.dma_start(out.rearrange("(a p) j -> p a j", p=P)[:, :, cols], res[:])
+
+        last = PACK - 1
+        magnetise(0)
+        field(0)
+        field(1)
+        numerator(0, 0, S)
+        field(2)
+        numerator(1, 0, S)
+        inv = [psum.tile([P, PACK, P], F32, name="inv%d" % b, tag="bank%d" % b) for b in range(BLOCKS)]
+        inverse(0, 0, S)
+        field(3)
+        numerator(2, 0, S)
+        inverse(1, 0, S)
+        for half in range(2):
+            numerator(last, half * S // 2, (half + 1) * S // 2)
+        inverse(2, 0, S)
+        for b in range(BLOCKS):
+            inverse(last, b * P, (b + 1) * P)
+        for t in range(PACK):
+            product(t)
+        for b in range(BLOCKS):
+            coils(b)

@@ -39,22 +39,22 @@ def tile_picked_yhystr_loss_p_kernel(
             nc.sync.dma_start(tile[:], src)
             return tile
 
-        def clear_plane(name, src, engine):
+        def clear_plane(name, src):
             passes, rows, width = src.shape
-            plane = keep.tile([P, passes * width], U8, name=name, align_bytes=64)
-            engine.memset(plane[:].bitcast(I32), 0)
+            plane = keep.tile([P, passes * width], U8, name=name, tag=name, align_bytes=64)
+            nc.gpsimd.memset(plane[:].bitcast(I32), 0)
             return plane
 
-        def load_scales(plane, src, queue):
+        def load_scales(plane, src):
             for q in range(4):
-                queue.dma_start(
+                nc.sync.dma_start(
                     plane[32 * q : 32 * q + 4, : src.shape[0] * src.shape[2]].bitcast(I32).rearrange("r (o c) -> r o c", o=src.shape[0]),
                     src[:, 4 * q : 4 * q + 4, :].bitcast(I32).rearrange("o r c -> r o c"),
                 )
 
         def load_words(name, src):
             passes, rows, width = src.shape
-            words = keep.tile([P, passes * width], U8, name=name, align_bytes=64)
+            words = keep.tile([P, passes * width], U8, name=name, tag=name, align_bytes=64)
             nc.sync.dma_start(
                 words[:].bitcast(I32).rearrange("p (o c) -> p o c", o=passes),
                 src.bitcast(I32).rearrange("o p c -> p o c"),
@@ -80,51 +80,54 @@ def tile_picked_yhystr_loss_p_kernel(
                 plane[:].rearrange("p (o m t) -> p o t m", o=PASSES, t=PACK),
             )
 
-        w2_plane = clear_plane("w2_plane", w2_scales, nc.gpsimd)
-        x_plane = clear_plane("x_plane", x_scales, nc.vector)
-        w1_plane = clear_plane("w1_plane", w1_scales, nc.vector)
-        w3_plane = clear_plane("w3_plane", w3_scales, nc.vector)
+        x_plane = clear_plane("x_plane", x_scales)
+        w2_plane = clear_plane("w2_plane", w2_scales)
+        w1_plane = clear_plane("w1_plane", w1_scales)
+        w3_plane = clear_plane("w3_plane", w3_scales)
         picks = load_list("picks", offs)
+        load_scales(x_plane, x_scales)
         w2_raw = load_words("w2_raw", w2_words)
+        x_table = [load_table(0)]
         first = load_list("first", nn1)
-        second = load_list("second", nn2)
-        load_scales(x_plane, x_scales, nc.sync)
-        load_scales(w2_plane, w2_scales, nc.gpsimd)
-        load_scales(w1_plane, w1_scales, nc.gpsimd)
-        x_table = [load_table(o) for o in range(PASSES)]
+        load_scales(w2_plane, w2_scales)
+        x_table.append(load_table(1))
         w1_raw = load_words("w1_raw", w1_words)
+        second = load_list("second", nn2)
+        load_scales(w1_plane, w1_scales)
         kpin_sb = keep.tile([P, PACK], F32)
         unit_sb = keep.tile([P, PACK], F32)
         nc.sync.dma_start(kpin_sb[:], kpin.rearrange("(p t) o -> p (t o)", t=PACK))
         nc.sync.dma_start(unit_sb[:], unit.rearrange("(p t) o -> p (t o)", t=PACK))
         w3_sb = load_words("w3_sb", w3_words)
-        load_scales(w3_plane, w3_scales, nc.sync)
+        load_scales(w3_plane, w3_scales)
 
         ident = keep.tile([P, P], F32)
         make_identity(nc, ident[:])
-        mag = [keep.tile([P, S + SPARE], F32, name="mag%d" % t) for t in range(PACK)]
-        for t in range(PACK):
-            nc.gpsimd.memset(mag[t][:, S:], 0.0)
-
         x_bytes = [keep.tile([P, S], U8, name="x_bytes%d" % o, align_bytes=64) for o in range(PASSES)]
         x_codes = [keep.tile([P, S], U32, name="x_codes%d" % o, align_bytes=64) for o in range(PASSES)]
         w2_codes = deal_words("w2_codes", w2_raw)
         w2_bytes = keep.tile([P, PASSES * H], U8, align_bytes=64)
         for o in range(PASSES):
             nc.vector.tensor_copy(x_bytes[o][:], x_plane[:, o * T : (o + 1) * T].indirect(picks[:]))
+        nc.vector.tensor_copy(x_codes[0][:], x_table[0][:].indirect(picks[:]))
         deal_scales(w2_bytes, w2_plane)
-        for o in range(PASSES):
-            nc.vector.tensor_copy(x_codes[o][:], x_table[o][:].indirect(picks[:]))
+        nc.vector.tensor_copy(x_codes[1][:], x_table[1][:].indirect(picks[:]))
         w1_codes = deal_words("w1_codes", w1_raw)
         w1_bytes = keep.tile([P, PASSES * H], U8, tag="table1", align_bytes=64)
         deal_scales(w1_bytes, w1_plane)
+        mag = [
+            keep.tile([P, S + SPARE], F32, name="mag%d" % t, tag="w1_raw" if t == 0 else "mag%d" % t, align_bytes=64)
+            for t in range(PACK)
+        ]
+        for t in range(PACK):
+            nc.gpsimd.memset(mag[t][:, S:], 0.0)
         gain = keep.tile([P, PACK], F32)
         nc.gpsimd.tensor_tensor(gain[:], kpin_sb[:], unit_sb[:], ALU.mult)
 
-        def first_pass(acc, codes, scale_bytes, t, o):
+        def first_pass(bank, codes, scale_bytes, t, o):
             col = (o * PACK + t) * P
             nc.tensor.matmul_mx(
-                out=acc[:],
+                out=bank[:],
                 lhsT=codes[:, 2 * col : 2 * (col + P)].bitcast(FP4X4),
                 lhsT_scale=scale_bytes[:, col : col + P],
                 rhs=x_codes[o][:].bitcast(FP8X4),
@@ -133,12 +136,13 @@ def tile_picked_yhystr_loss_p_kernel(
                 stop=(o == PASSES - 1),
             )
 
-        mg = [psum.tile([P, S], F32, name="mg%d" % t, tag="bank%d" % t) for t in range(PACK)]
+        acc = [psum.tile([P, S], F32, name="acc%d" % i) for i in range(2)]
 
         def magnetise(t):
+            mg = psum.tile([P, S], F32, name="mg%d" % t, tag="bank%d" % t) if t < 2 else acc[t % 2]
             for o in range(PASSES):
-                first_pass(mg[t], w2_codes, w2_bytes, t, o)
-            nc.scalar.activation(mag[t][:, :S], mg[t][:], ACT.Tanh)
+                first_pass(mg, w2_codes, w2_bytes, t, o)
+            nc.scalar.activation(mag[t][:, :S], mg[:], ACT.Tanh)
 
         heff = keep.tile([P, PACK, S], F32)
         absh = keep.tile([P, PACK, S], F32)
@@ -148,14 +152,14 @@ def tile_picked_yhystr_loss_p_kernel(
         def field(t):
             m1 = ring.tile([P, S], F32, name="m1")
             nc.scalar.activation(m1[:], mag[t][:].indirect(first[:]), ACT.Copy)
-            if t + 1 < PACK:
-                magnetise(t + 1)
-            hf = psum2.tile([P, S], F32, name="hf", tag="acc")
+            if t == 0:
+                magnetise(1)
+            hf = acc[t % 2] if t < PACK - 1 else psum2.tile([P, S], F32, name="hf", tag="den")
             for o in range(PASSES):
                 first_pass(hf, w1_codes, w1_bytes, t, o)
             both = keep.tile([P, S], F32, name="both")
             if t == 0:
-                m2 = keep.tile([P, S], F32)
+                m2 = keep.tile([P, S], F32, tag="w1_plane", align_bytes=64)
                 for half in range(2):
                     nc.vector.tensor_copy(
                         m2[:, half * S // 2 : (half + 1) * S // 2],
@@ -167,6 +171,8 @@ def tile_picked_yhystr_loss_p_kernel(
             own = ring.tile([P, S], F32, name="own")
             nc.vector.scalar_tensor_tensor(own[:], mag[t][:, :S], 0.6, hf[:], ALU.mult, ALU.add)
             nc.vector.scalar_tensor_tensor(heff[:, t, :], both[:], 0.3, own[:], ALU.mult, ALU.add)
+            if t + 2 < PACK:
+                magnetise(t + 2)
             nc.scalar.activation(absh[:, t, :], heff[:, t, :], ACT.Abs, scale=0.4)
 
         def numerator(t, lo, hi):
@@ -178,7 +184,7 @@ def tile_picked_yhystr_loss_p_kernel(
             width = hi - lo
             absn = ring.tile([P, width], F32, name="absn")
             nc.scalar.activation(absn[:], num[:, t, lo:hi], ACT.Abs)
-            den = psum2.tile([P, width], F32, name="den", tag="den")
+            den = acc[1] if t == 0 else psum2.tile([P, width], F32, name="den", tag="den")
             for c in range(0, width, P):
                 nc.tensor.matmul(den[:, c : c + P], absh[:, t, lo + c : lo + c + P], ident[:], start=True, stop=False, is_transpose=True)
                 nc.tensor.matmul(den[:, c : c + P], absn[:, c : c + P], ident[:], start=False, stop=True, is_transpose=True)
@@ -204,10 +210,10 @@ def tile_picked_yhystr_loss_p_kernel(
             codes = ring.tile([P, P], U32, name="codes", align_bytes=64)
             scale_bytes = ring.tile([P, P], U8, name="scale_bytes", align_bytes=64)
             nc.vector.quantize_mx(out=codes[:].bitcast(FP8X4), scales=scale_bytes[:], in_=hid[:])
-            acc = psum2.tile([P, N // P, P], F32, name="acc", tag="acc")
+            coil = acc[b % 2][:, :N].rearrange("p (a j) -> p a j", j=P)
             for a in range(N // P):
                 nc.tensor.matmul_mx(
-                    out=acc[:, a, :],
+                    out=coil[:, a, :],
                     lhsT=w3_sb[:, 2 * a * P : 2 * (a + 1) * P].bitcast(FP4X4),
                     lhsT_scale=w3_plane[:, a * P : (a + 1) * P],
                     rhs=codes[:].bitcast(FP8X4),
@@ -216,7 +222,7 @@ def tile_picked_yhystr_loss_p_kernel(
                     stop=True,
                 )
             res = keep.tile([P, N // P, P], F32, name="res%d" % b)
-            nc.scalar.copy(res[:], acc[:])
+            nc.scalar.copy(res[:], coil)
             nc.sync.dma_start(out.rearrange("(a p) j -> p a j", p=P)[:, :, cols], res[:])
 
         last = PACK - 1

@@ -74,26 +74,28 @@ def tile_picked_yhystr_loss_p_kernel(
             )
             return dealt
 
-        def deal_scales(dealt, plane):
+        def deal_scales(dealt, plane, tiles):
             nc.vector.tensor_copy(
-                dealt[:].rearrange("p (o t m) -> p o t m", o=PASSES, t=PACK),
-                plane[:].rearrange("p (o m t) -> p o t m", o=PASSES, t=PACK),
+                dealt[:].rearrange("p (o t m) -> p o t m", o=PASSES, t=PACK)[:, :, tiles, :],
+                plane[:].rearrange("p (o m t) -> p o t m", o=PASSES, t=PACK)[:, :, tiles, :],
             )
 
-        x_plane = clear_plane("x_plane", x_scales)
+        x_plane = keep.tile([P, PASSES * T], U8, align_bytes=64)
+        share = PASSES * T // 4
+        nc.gpsimd.memset(x_plane[:, :share].bitcast(I32), 0)
+        nc.vector.memset(x_plane[:, share:].bitcast(I32), 0)
         w2_plane = clear_plane("w2_plane", w2_scales)
         w1_plane = clear_plane("w1_plane", w1_scales)
         w3_plane = clear_plane("w3_plane", w3_scales)
         picks = load_list("picks", offs)
-        load_scales(x_plane, x_scales)
         w2_raw = load_words("w2_raw", w2_words)
-        x_table = [load_table(0)]
-        first = load_list("first", nn1)
-        load_scales(w2_plane, w2_scales)
-        x_table.append(load_table(1))
         w1_raw = load_words("w1_raw", w1_words)
-        second = load_list("second", nn2)
+        load_scales(x_plane, x_scales)
+        x_table = [load_table(o) for o in range(PASSES)]
+        load_scales(w2_plane, w2_scales)
         load_scales(w1_plane, w1_scales)
+        first = load_list("first", nn1)
+        second = load_list("second", nn2)
         kpin_sb = keep.tile([P, PACK], F32)
         unit_sb = keep.tile([P, PACK], F32)
         nc.sync.dma_start(kpin_sb[:], kpin.rearrange("(p t) o -> p (t o)", t=PACK))
@@ -110,15 +112,13 @@ def tile_picked_yhystr_loss_p_kernel(
         for o in range(PASSES):
             nc.vector.tensor_copy(x_bytes[o][:], x_plane[:, o * T : (o + 1) * T].indirect(picks[:]))
         nc.vector.tensor_copy(x_codes[0][:], x_table[0][:].indirect(picks[:]))
-        deal_scales(w2_bytes, w2_plane)
         nc.vector.tensor_copy(x_codes[1][:], x_table[1][:].indirect(picks[:]))
+        deal_scales(w2_bytes, w2_plane, slice(0, 1))
+        deal_scales(w2_bytes, w2_plane, slice(1, PACK))
         w1_codes = deal_words("w1_codes", w1_raw)
         w1_bytes = keep.tile([P, PASSES * H], U8, tag="table1", align_bytes=64)
-        deal_scales(w1_bytes, w1_plane)
-        mag = [
-            keep.tile([P, S + SPARE], F32, name="mag%d" % t, tag="w1_raw" if t == 0 else "mag%d" % t, align_bytes=64)
-            for t in range(PACK)
-        ]
+        deal_scales(w1_bytes, w1_plane, slice(0, PACK))
+        mag = [keep.tile([P, S + SPARE], F32, name="mag%d" % t) for t in range(PACK)]
         for t in range(PACK):
             nc.gpsimd.memset(mag[t][:, S:], 0.0)
         gain = keep.tile([P, PACK], F32)
@@ -147,7 +147,6 @@ def tile_picked_yhystr_loss_p_kernel(
         heff = keep.tile([P, PACK, S], F32)
         absh = keep.tile([P, PACK, S], F32)
         num = keep.tile([P, PACK, S], F32)
-        prod = keep.tile([P, PACK, S], F32)
 
         def field(t):
             m1 = ring.tile([P, S], F32, name="m1")
@@ -157,7 +156,7 @@ def tile_picked_yhystr_loss_p_kernel(
             hf = acc[t % 2] if t < PACK - 1 else psum2.tile([P, S], F32, name="hf", tag="den")
             for o in range(PASSES):
                 first_pass(hf, w1_codes, w1_bytes, t, o)
-            both = keep.tile([P, S], F32, name="both")
+            both = keep.tile([P, S], F32, name="both", tag="both")
             if t == 0:
                 m2 = keep.tile([P, S], F32, tag="w1_plane", align_bytes=64)
                 for half in range(2):
@@ -180,20 +179,30 @@ def tile_picked_yhystr_loss_p_kernel(
             nc.vector.scalar_tensor_tensor(pull[:], absh[:, t, lo:hi], 0.32, mag[t][:, lo:hi], ALU.add, ALU.mult)
             nc.vector.scalar_tensor_tensor(num[:, t, lo:hi], pull[:], -2.5, heff[:, t, lo:hi], ALU.mult, ALU.add)
 
-        def inverse(t, lo, hi):
-            width = hi - lo
-            absn = ring.tile([P, width], F32, name="absn")
-            nc.scalar.activation(absn[:], num[:, t, lo:hi], ACT.Abs)
-            den = acc[1] if t == 0 else psum2.tile([P, width], F32, name="den", tag="den")
-            for c in range(0, width, P):
-                nc.tensor.matmul(den[:, c : c + P], absh[:, t, lo + c : lo + c + P], ident[:], start=True, stop=False, is_transpose=True)
-                nc.tensor.matmul(den[:, c : c + P], absn[:, c : c + P], ident[:], start=False, stop=True, is_transpose=True)
+        def inverse(den, absn, pieces):
+            for i, (t, b) in enumerate(pieces):
+                block = slice(i * P, (i + 1) * P)
+                nc.tensor.matmul(den[:, block], absh[:, t, b * P : (b + 1) * P], ident[:], start=True, stop=False, is_transpose=True)
+                nc.tensor.matmul(den[:, block], absn[:, block], ident[:], start=False, stop=True, is_transpose=True)
+            width = len(pieces) * P
             root = ring.tile([P, width], F32, name="root")
-            nc.scalar.activation(root[:], den[:], ACT.Abs_reciprocal_sqrt, bias=0.32)
+            nc.scalar.activation(root[:], den[:, :width], ACT.Abs_reciprocal_sqrt, bias=0.32)
             turned = ring.tile([P, width], F32, name="turned")
             nc.scalar.activation(turned[:], root[:], ACT.Square)
-            for c in range(0, width, P):
-                nc.tensor.transpose(inv[(lo + c) // P][:, t, :], turned[:, c : c + P], ident[:])
+            for i, (t, b) in enumerate(pieces):
+                nc.tensor.transpose(inv[b][:, t, :], turned[:, i * P : (i + 1) * P], ident[:])
+
+        def inverse_of_tile(t):
+            absn = ring.tile([P, S], F32, name="absn")
+            nc.scalar.activation(absn[:], num[:, t, :], ACT.Abs)
+            den = acc[1] if t == 0 else psum2.tile([P, S], F32, name="den", tag="den")
+            inverse(den, absn, [(t, b) for b in range(BLOCKS)])
+
+        def inverse_of_block(b):
+            absn = ring.tile([P, 2 * P], F32, name="absn")
+            nc.scalar.activation(absn[:].rearrange("p (t j) -> p t j", t=2), num[:, 2:, b * P : (b + 1) * P], ACT.Abs)
+            den = psum2.tile([P, 2 * P], F32, name="den", tag="den")
+            inverse(den, absn, [(2, b), (3, b)])
 
         def product(t):
             nc.vector.scalar_tensor_tensor(prod[:, t, :], heff[:, t, :], gain[:, t : t + 1], num[:, t, :], ALU.mult, ALU.mult)
@@ -233,15 +242,15 @@ def tile_picked_yhystr_loss_p_kernel(
         field(2)
         numerator(1, 0, S)
         inv = [psum.tile([P, PACK, P], F32, name="inv%d" % b, tag="bank%d" % b) for b in range(BLOCKS)]
-        inverse(0, 0, S)
+        inverse_of_tile(0)
         field(3)
         numerator(2, 0, S)
-        inverse(1, 0, S)
         for half in range(2):
             numerator(last, half * S // 2, (half + 1) * S // 2)
-        inverse(2, 0, S)
+        inverse_of_tile(1)
+        prod = keep.tile([P, PACK, S], F32, tag="both")
         for b in range(BLOCKS):
-            inverse(last, b * P, (b + 1) * P)
+            inverse_of_block(b)
         for t in range(PACK):
             product(t)
         for b in range(BLOCKS):

@@ -194,7 +194,10 @@ def tile_picked_yhystr_loss_p_kernel(
 
         def inverse_of_tile(t):
             absn = ring.tile([P, S], F32, name="absn")
-            nc.scalar.activation(absn[:], num[:, t, :], ACT.Abs)
+            if t == 0:
+                nc.scalar.activation(absn[:], num[:, t, :], ACT.Abs)
+            else:
+                nc.vector.scalar_tensor_tensor(absn[:], num[:, t, :], -1.0, num[:, t, :], ALU.mult, ALU.max)
             den = acc[1] if t == 0 else psum2.tile([P, S], F32, name="den", tag="den")
             inverse(den, absn, [(t, b) for b in range(BLOCKS)])
 
@@ -211,9 +214,9 @@ def tile_picked_yhystr_loss_p_kernel(
             cols = slice(b * P, (b + 1) * P)
             hid = ring.tile([P, P * PACK], BF16, name="hid", align_bytes=64)
             nc.vector.tensor_tensor(
-                hid[:].rearrange("p (c i t) -> p c t i", i=4, t=PACK),
-                prod[:, :, cols].rearrange("p t (c i) -> p c t i", i=4),
-                inv[b][:].rearrange("p t (c i) -> p c t i", i=4),
+                hid[:].rearrange("p (c t) -> p c t", t=PACK),
+                prod[:, :, cols].rearrange("p t c -> p c t"),
+                inv[b][:].rearrange("p t c -> p c t"),
                 ALU.mult,
             )
             codes = ring.tile([P, P], U32, name="codes", align_bytes=64)

@@ -22,6 +22,10 @@ PACK = 4
 PASSES = K // (P * PACK)
 SPARE = 8
 BLOCKS = S // P
+HALF = S // 2
+HALF_COLS = HALF // 16
+QUADRANTS = 4
+WARM_UP = 4
 
 
 def tile_picked_yhystr_loss_p_kernel(
@@ -40,21 +44,20 @@ def tile_picked_yhystr_loss_p_kernel(
             return tile
 
         def clear_plane(name, src):
-            passes, rows, width = src.shape
-            plane = keep.tile([P, passes * width], U8, name=name, tag=name, align_bytes=64)
+            plane = keep.tile([P, src.shape[0] * src.shape[2]], U8, name=name, tag=name, align_bytes=64)
             nc.gpsimd.memset(plane[:].bitcast(I32), 0)
             return plane
 
         def load_scales(plane, src):
-            for q in range(4):
+            for q in range(QUADRANTS):
                 nc.sync.dma_start(
-                    plane[32 * q : 32 * q + 4, : src.shape[0] * src.shape[2]].bitcast(I32).rearrange("r (o c) -> r o c", o=src.shape[0]),
+                    plane[32 * q : 32 * q + 4, :].bitcast(I32).rearrange("r (o c) -> r o c", o=src.shape[0]),
                     src[:, 4 * q : 4 * q + 4, :].bitcast(I32).rearrange("o r c -> r o c"),
                 )
 
         def load_words(name, src):
-            passes, rows, width = src.shape
-            words = keep.tile([P, passes * width], U8, name=name, tag=name, align_bytes=64)
+            passes = src.shape[0]
+            words = keep.tile([P, passes * src.shape[2]], U8, name=name, tag=name, align_bytes=64)
             nc.sync.dma_start(
                 words[:].bitcast(I32).rearrange("p (o c) -> p o c", o=passes),
                 src.bitcast(I32).rearrange("o p c -> p o c"),
@@ -87,6 +90,7 @@ def tile_picked_yhystr_loss_p_kernel(
         w2_plane = clear_plane("w2_plane", w2_scales)
         w1_plane = clear_plane("w1_plane", w1_scales)
         w3_plane = clear_plane("w3_plane", w3_scales)
+
         picks = load_list("picks", offs)
         w2_raw = load_words("w2_raw", w2_words)
         w1_raw = load_words("w1_raw", w1_words)
@@ -94,8 +98,8 @@ def tile_picked_yhystr_loss_p_kernel(
         x_table = [load_table(o) for o in range(PASSES)]
         load_scales(w2_plane, w2_scales)
         load_scales(w1_plane, w1_scales)
-        first = load_list("first", nn1)
-        second = load_list("second", nn2)
+        near1 = load_list("near1", nn1)
+        near2 = load_list("near2", nn2)
         kpin_sb = keep.tile([P, PACK], F32)
         unit_sb = keep.tile([P, PACK], F32)
         nc.sync.dma_start(kpin_sb[:], kpin.rearrange("(p t) o -> p (t o)", t=PACK))
@@ -105,6 +109,7 @@ def tile_picked_yhystr_loss_p_kernel(
 
         ident = keep.tile([P, P], F32)
         make_identity(nc, ident[:])
+
         x_bytes = [keep.tile([P, S], U8, name="x_bytes%d" % o, align_bytes=64) for o in range(PASSES)]
         x_codes = [keep.tile([P, S], U32, name="x_codes%d" % o, align_bytes=64) for o in range(PASSES)]
         w2_codes = deal_words("w2_codes", w2_raw)
@@ -112,28 +117,42 @@ def tile_picked_yhystr_loss_p_kernel(
         for o in range(PASSES):
             nc.vector.tensor_copy(x_bytes[o][:], x_plane[:, o * T : (o + 1) * T].indirect(picks[:]))
         nc.vector.tensor_copy(x_codes[0][:], x_table[0][:].indirect(picks[:]))
-        nc.vector.tensor_copy(x_codes[1][:], x_table[1][:].indirect(picks[:]))
+        nc.vector.tensor_copy(x_codes[1][:, :HALF], x_table[1][:].indirect(picks[:, :HALF_COLS]))
         deal_scales(w2_bytes, w2_plane, slice(0, 1))
+        nc.vector.tensor_copy(x_codes[1][:, HALF:], x_table[1][:].indirect(picks[:, HALF_COLS:]))
         deal_scales(w2_bytes, w2_plane, slice(1, PACK))
         w1_codes = deal_words("w1_codes", w1_raw)
         w1_bytes = keep.tile([P, PASSES * H], U8, tag="table1", align_bytes=64)
         deal_scales(w1_bytes, w1_plane, slice(0, PACK))
+
         mag = [keep.tile([P, S + SPARE], F32, name="mag%d" % t) for t in range(PACK)]
         for t in range(PACK):
             nc.gpsimd.memset(mag[t][:, S:], 0.0)
         gain = keep.tile([P, PACK], F32)
         nc.gpsimd.tensor_tensor(gain[:], kpin_sb[:], unit_sb[:], ALU.mult)
 
-        def first_pass(bank, codes, scale_bytes, t, o):
+        def cell_pass(bank, w_codes, w_bytes, t, o):
             col = (o * PACK + t) * P
             nc.tensor.matmul_mx(
                 out=bank[:],
-                lhsT=codes[:, 2 * col : 2 * (col + P)].bitcast(FP4X4),
-                lhsT_scale=scale_bytes[:, col : col + P],
+                lhsT=w_codes[:, 2 * col : 2 * (col + P)].bitcast(FP4X4),
+                lhsT_scale=w_bytes[:, col : col + P],
                 rhs=x_codes[o][:].bitcast(FP8X4),
                 rhs_scale=x_bytes[o][:],
                 start=(o == 0),
                 stop=(o == PASSES - 1),
+            )
+
+        unread = psum.tile([P, S], F32, tag="bank3")
+        for i in range(WARM_UP):
+            nc.tensor.matmul_mx(
+                out=unread[:],
+                lhsT=w2_codes[:, : 2 * P].bitcast(FP4X4),
+                lhsT_scale=x_bytes[0][:, :P],
+                rhs=x_codes[0][:].bitcast(FP8X4),
+                rhs_scale=x_bytes[0][:],
+                start=True,
+                stop=True,
             )
 
         acc = [psum.tile([P, S], F32, name="acc%d" % i) for i in range(2)]
@@ -141,7 +160,7 @@ def tile_picked_yhystr_loss_p_kernel(
         def magnetise(t):
             mg = psum.tile([P, S], F32, name="mg%d" % t, tag="bank%d" % t) if t < 2 else acc[t % 2]
             for o in range(PASSES):
-                first_pass(mg, w2_codes, w2_bytes, t, o)
+                cell_pass(mg, w2_codes, w2_bytes, t, o)
             nc.scalar.activation(mag[t][:, :S], mg[:], ACT.Tanh)
 
         heff = keep.tile([P, PACK, S], F32)
@@ -150,23 +169,23 @@ def tile_picked_yhystr_loss_p_kernel(
 
         def field(t):
             m1 = ring.tile([P, S], F32, name="m1")
-            nc.scalar.activation(m1[:], mag[t][:].indirect(first[:]), ACT.Copy)
+            nc.scalar.activation(m1[:], mag[t][:].indirect(near1[:]), ACT.Copy)
             if t == 0:
                 magnetise(1)
             hf = acc[t % 2] if t < PACK - 1 else psum2.tile([P, S], F32, name="hf", tag="den")
             for o in range(PASSES):
-                first_pass(hf, w1_codes, w1_bytes, t, o)
+                cell_pass(hf, w1_codes, w1_bytes, t, o)
             both = keep.tile([P, S], F32, name="both", tag="both")
             if t == 0:
                 m2 = keep.tile([P, S], F32, tag="w1_plane", align_bytes=64)
                 for half in range(2):
                     nc.vector.tensor_copy(
-                        m2[:, half * S // 2 : (half + 1) * S // 2],
-                        mag[t][:].indirect(second[:, half * S // 32 : (half + 1) * S // 32]),
+                        m2[:, half * HALF : (half + 1) * HALF],
+                        mag[t][:].indirect(near2[:, half * HALF_COLS : (half + 1) * HALF_COLS]),
                     )
                 nc.vector.tensor_tensor(both[:], m2[:], m1[:], ALU.add)
             else:
-                nc.vector.tensor_tensor(both[:], mag[t][:].indirect(second[:]), m1[:], ALU.add)
+                nc.vector.tensor_tensor(both[:], mag[t][:].indirect(near2[:]), m1[:], ALU.add)
             own = ring.tile([P, S], F32, name="own")
             nc.vector.scalar_tensor_tensor(own[:], mag[t][:, :S], 0.6, hf[:], ALU.mult, ALU.add)
             nc.vector.scalar_tensor_tensor(heff[:, t, :], both[:], 0.3, own[:], ALU.mult, ALU.add)
@@ -219,17 +238,17 @@ def tile_picked_yhystr_loss_p_kernel(
                 inv[b][:].rearrange("p t c -> p c t"),
                 ALU.mult,
             )
-            codes = ring.tile([P, P], U32, name="codes", align_bytes=64)
-            scale_bytes = ring.tile([P, P], U8, name="scale_bytes", align_bytes=64)
-            nc.vector.quantize_mx(out=codes[:].bitcast(FP8X4), scales=scale_bytes[:], in_=hid[:])
+            hid_codes = ring.tile([P, P], U32, name="hid_codes", align_bytes=64)
+            hid_bytes = ring.tile([P, P], U8, name="hid_bytes", align_bytes=64)
+            nc.vector.quantize_mx(out=hid_codes[:].bitcast(FP8X4), scales=hid_bytes[:], in_=hid[:])
             coil = acc[b % 2][:, :N].rearrange("p (a j) -> p a j", j=P)
             for a in range(N // P):
                 nc.tensor.matmul_mx(
                     out=coil[:, a, :],
                     lhsT=w3_sb[:, 2 * a * P : 2 * (a + 1) * P].bitcast(FP4X4),
                     lhsT_scale=w3_plane[:, a * P : (a + 1) * P],
-                    rhs=codes[:].bitcast(FP8X4),
-                    rhs_scale=scale_bytes[:],
+                    rhs=hid_codes[:].bitcast(FP8X4),
+                    rhs_scale=hid_bytes[:],
                     start=True,
                     stop=True,
                 )
@@ -237,7 +256,6 @@ def tile_picked_yhystr_loss_p_kernel(
             nc.scalar.copy(res[:], coil)
             nc.sync.dma_start(out.rearrange("(a p) j -> p a j", p=P)[:, :, cols], res[:])
 
-        last = PACK - 1
         magnetise(0)
         field(0)
         field(1)
@@ -249,7 +267,7 @@ def tile_picked_yhystr_loss_p_kernel(
         field(3)
         numerator(2, 0, S)
         for half in range(2):
-            numerator(last, half * S // 2, (half + 1) * S // 2)
+            numerator(3, half * HALF, (half + 1) * HALF)
         inverse_of_tile(1)
         prod = keep.tile([P, PACK, S], F32, tag="both")
         for b in range(BLOCKS):

from contextlib import ExitStack

import concourse.mybir as mybir
from concourse.masks import make_identity

K, T, S, N, H = 1024, 2048, 512, 256, 512
FLOPS = 2 * (2 * K * H * S + H * N * S)

F32 = mybir.dt.float32
BF16 = mybir.dt.bfloat16
I32 = mybir.dt.int32
U32 = mybir.dt.uint32
U16 = mybir.dt.uint16
U8 = mybir.dt.uint8
FP8X4 = mybir.dt.float8_e4m3fn_x4
FP4X4 = mybir.dt.float4_e2m1fn_x4
ALU = mybir.AluOpType
ACT = mybir.ActivationFunctionType

P = 128
PACK = 4
PASSES = K // (P * PACK)
SPARE = 8
BLOCKS = S // P
HALF = S // 2
HALF_COLS = HALF // 16
QUADRANTS = 4
WARM_UP = 4


def tile_picked_yhystr_loss_p_kernel(
    tc, x_words, x_scales, w1_words, w1_scales, w2_words, w2_scales, kpin, unit, w3_words, w3_scales, offs, nn1, nn2, out
):
    nc = tc.nc
    with ExitStack() as ctx:
        keep = ctx.enter_context(tc.tile_pool(name="keep", bufs=1))
        ring = ctx.enter_context(tc.tile_pool(name="ring", bufs=2))
        psum = ctx.enter_context(tc.psum_pool(name="psum", bufs=1))
        psum2 = ctx.enter_context(tc.psum_pool(name="psum2", bufs=2))

        def load_list(name, src):
            tile = keep.tile([P, S // 16], U16, name=name)
            nc.sync.dma_start(tile[:], src)
            return tile

        def clear_plane(name, src):
            plane = keep.tile([P, src.shape[0] * src.shape[2]], U8, name=name, tag=name, align_bytes=64)
            nc.gpsimd.memset(plane[:].bitcast(I32), 0)
            return plane

        def load_scales(plane, src):
            for q in range(QUADRANTS):
                nc.sync.dma_start(
                    plane[32 * q : 32 * q + 4, :].bitcast(I32).rearrange("r (o c) -> r o c", o=src.shape[0]),
                    src[:, 4 * q : 4 * q + 4, :].bitcast(I32).rearrange("o r c -> r o c"),
                )

        def load_words(name, src):
            passes = src.shape[0]
            words = keep.tile([P, passes * src.shape[2]], U8, name=name, tag=name, align_bytes=64)
            nc.sync.dma_start(
                words[:].bitcast(I32).rearrange("p (o c) -> p o c", o=passes),
                src.bitcast(I32).rearrange("o p c -> p o c"),
            )
            return words

        def load_table(o):
            table = keep.tile([P, T], U32, name="x_table%d" % o, tag="table%d" % o, align_bytes=64)
            nc.sync.dma_start(table[:].bitcast(I32), x_words[o].rearrange("p c r -> p (c r)").bitcast(I32))
            return table

        def deal_words(name, words):
            dealt = keep.tile([P, PASSES * H * 2], U8, name=name, align_bytes=64)
            nc.scalar.copy(
                dealt[:].bitcast(U16).rearrange("p (o t m) -> p o t m", o=PASSES, t=PACK),
                words[:].bitcast(U16).rearrange("p (o m t) -> p o t m", o=PASSES, t=PACK),
            )
            return dealt

        def deal_scales(dealt, plane, tiles):
            nc.vector.tensor_copy(
                dealt[:].rearrange("p (o t m) -> p o t m", o=PASSES, t=PACK)[:, :, tiles, :],
                plane[:].rearrange("p (o m t) -> p o t m", o=PASSES, t=PACK)[:, :, tiles, :],
            )

        x_plane = keep.tile([P, PASSES * T], U8, align_bytes=64)
        share = PASSES * T // 4
        nc.gpsimd.memset(x_plane[:, :share].bitcast(I32), 0)
        nc.vector.memset(x_plane[:, share:].bitcast(I32), 0)
        w2_plane = clear_plane("w2_plane", w2_scales)
        w1_plane = clear_plane("w1_plane", w1_scales)
        w3_plane = clear_plane("w3_plane", w3_scales)

        picks = load_list("picks", offs)
        w2_raw = load_words("w2_raw", w2_words)
        w1_raw = load_words("w1_raw", w1_words)
        load_scales(x_plane, x_scales)
        x_table = [load_table(o) for o in range(PASSES)]
        load_scales(w2_plane, w2_scales)
        load_scales(w1_plane, w1_scales)
        near1 = load_list("near1", nn1)
        near2 = load_list("near2", nn2)
        kpin_sb = keep.tile([P, PACK], F32)
        unit_sb = keep.tile([P, PACK], F32)
        nc.sync.dma_start(kpin_sb[:], kpin.rearrange("(p t) o -> p (t o)", t=PACK))
        nc.sync.dma_start(unit_sb[:], unit.rearrange("(p t) o -> p (t o)", t=PACK))
        w3_sb = load_words("w3_sb", w3_words)
        load_scales(w3_plane, w3_scales)

        ident = keep.tile([P, P], F32)
        make_identity(nc, ident[:])

        x_bytes = [keep.tile([P, S], U8, name="x_bytes%d" % o, align_bytes=64) for o in range(PASSES)]
        x_codes = [keep.tile([P, S], U32, name="x_codes%d" % o, align_bytes=64) for o in range(PASSES)]
        w2_codes = deal_words("w2_codes", w2_raw)
        w2_bytes = keep.tile([P, PASSES * H], U8, align_bytes=64)
        for o in range(PASSES):
            nc.vector.tensor_copy(x_bytes[o][:], x_plane[:, o * T : (o + 1) * T].indirect(picks[:]))
        nc.vector.tensor_copy(x_codes[0][:], x_table[0][:].indirect(picks[:]))
        nc.vector.tensor_copy(x_codes[1][:, :HALF], x_table[1][:].indirect(picks[:, :HALF_COLS]))
        deal_scales(w2_bytes, w2_plane, slice(0, 1))
        nc.vector.tensor_copy(x_codes[1][:, HALF:], x_table[1][:].indirect(picks[:, HALF_COLS:]))
        deal_scales(w2_bytes, w2_plane, slice(1, PACK))
        w1_codes = deal_words("w1_codes", w1_raw)
        w1_bytes = keep.tile([P, PASSES * H], U8, tag="table1", align_bytes=64)
        deal_scales(w1_bytes, w1_plane, slice(0, PACK))

        mag = [keep.tile([P, S + SPARE], F32, name="mag%d" % t) for t in range(PACK)]
        for t in range(PACK):
            nc.gpsimd.memset(mag[t][:, S:], 0.0)
        gain = keep.tile([P, PACK], F32)
        nc.gpsimd.tensor_tensor(gain[:], kpin_sb[:], unit_sb[:], ALU.mult)

        def cell_pass(bank, w_codes, w_bytes, t, o):
            col = (o * PACK + t) * P
            nc.tensor.matmul_mx(
                out=bank[:],
                lhsT=w_codes[:, 2 * col : 2 * (col + P)].bitcast(FP4X4),
                lhsT_scale=w_bytes[:, col : col + P],
                rhs=x_codes[o][:].bitcast(FP8X4),
                rhs_scale=x_bytes[o][:],
                start=(o == 0),
                stop=(o == PASSES - 1),
            )

        unread = psum.tile([P, S], F32, tag="bank3")
        for i in range(WARM_UP):
            nc.tensor.matmul_mx(
                out=unread[:],
                lhsT=w2_codes[:, : 2 * P].bitcast(FP4X4),
                lhsT_scale=x_bytes[0][:, :P],
                rhs=x_codes[0][:].bitcast(FP8X4),
                rhs_scale=x_bytes[0][:],
                start=True,
                stop=True,
            )

        acc = [psum.tile([P, S], F32, name="acc%d" % i) for i in range(2)]

        def magnetise(t):
            mg = psum.tile([P, S], F32, name="mg%d" % t, tag="bank%d" % t) if t < 2 else acc[t % 2]
            for o in range(PASSES):
                cell_pass(mg, w2_codes, w2_bytes, t, o)
            nc.scalar.activation(mag[t][:, :S], mg[:], ACT.Tanh)

        heff = keep.tile([P, PACK, S], F32)
        absh = keep.tile([P, PACK, S], F32)
        num = keep.tile([P, PACK, S], F32)

        def field(t):
            m1 = ring.tile([P, S], F32, name="m1")
            nc.scalar.activation(m1[:], mag[t][:].indirect(near1[:]), ACT.Copy)
            if t == 0:
                magnetise(1)
            hf = acc[t % 2] if t < PACK - 1 else psum2.tile([P, S], F32, name="hf", tag="den")
            for o in range(PASSES):
                cell_pass(hf, w1_codes, w1_bytes, t, o)
            both = keep.tile([P, S], F32, name="both", tag="both")
            if t == 0:
                m2 = keep.tile([P, S], F32, tag="w1_plane", align_bytes=64)
                for half in range(2):
                    nc.vector.tensor_copy(
                        m2[:, half * HALF : (half + 1) * HALF],
                        mag[t][:].indirect(near2[:, half * HALF_COLS : (half + 1) * HALF_COLS]),
                    )
                nc.vector.tensor_tensor(both[:], m2[:], m1[:], ALU.add)
            else:
                nc.vector.tensor_tensor(both[:], mag[t][:].indirect(near2[:]), m1[:], ALU.add)
            own = ring.tile([P, S], F32, name="own")
            nc.vector.scalar_tensor_tensor(own[:], mag[t][:, :S], 0.6, hf[:], ALU.mult, ALU.add)
            nc.vector.scalar_tensor_tensor(heff[:, t, :], both[:], 0.3, own[:], ALU.mult, ALU.add)
            if t + 2 < PACK:
                magnetise(t + 2)
            nc.scalar.activation(absh[:, t, :], heff[:, t, :], ACT.Abs, scale=0.4)

        def numerator(t, lo, hi):
            pull = ring.tile([P, hi - lo], F32, name="pull")
            nc.vector.scalar_tensor_tensor(pull[:], absh[:, t, lo:hi], 0.32, mag[t][:, lo:hi], ALU.add, ALU.mult)
            nc.vector.scalar_tensor_tensor(num[:, t, lo:hi], pull[:], -2.5, heff[:, t, lo:hi], ALU.mult, ALU.add)

        def inverse(den, absn, pieces):
            for i, (t, b) in enumerate(pieces):
                block = slice(i * P, (i + 1) * P)
                nc.tensor.matmul(den[:, block], absh[:, t, b * P : (b + 1) * P], ident[:], start=True, stop=False, is_transpose=True)
                nc.tensor.matmul(den[:, block], absn[:, block], ident[:], start=False, stop=True, is_transpose=True)
            width = len(pieces) * P
            root = ring.tile([P, width], F32, name="root")
            nc.scalar.activation(root[:], den[:, :width], ACT.Abs_reciprocal_sqrt, bias=0.32)
            turned = ring.tile([P, width], F32, name="turned")
            nc.scalar.activation(turned[:], root[:], ACT.Square)
            for i, (t, b) in enumerate(pieces):
                nc.tensor.transpose(inv[b][:, t, :], turned[:, i * P : (i + 1) * P], ident[:])

        def inverse_of_tile(t):
            absn = ring.tile([P, S], F32, name="absn")
            if t == 0:
                nc.scalar.activation(absn[:], num[:, t, :], ACT.Abs)
            else:
                nc.vector.scalar_tensor_tensor(absn[:], num[:, t, :], -1.0, num[:, t, :], ALU.mult, ALU.max)
            den = acc[1] if t == 0 else psum2.tile([P, S], F32, name="den", tag="den")
            inverse(den, absn, [(t, b) for b in range(BLOCKS)])

        def inverse_of_block(b):
            absn = ring.tile([P, 2 * P], F32, name="absn")
            nc.scalar.activation(absn[:].rearrange("p (t j) -> p t j", t=2), num[:, 2:, b * P : (b + 1) * P], ACT.Abs)
            den = psum2.tile([P, 2 * P], F32, name="den", tag="den")
            inverse(den, absn, [(2, b), (3, b)])

        def product(t):
            nc.vector.scalar_tensor_tensor(prod[:, t, :], heff[:, t, :], gain[:, t : t + 1], num[:, t, :], ALU.mult, ALU.mult)

        def coils(b):
            cols = slice(b * P, (b + 1) * P)
            hid = ring.tile([P, P * PACK], BF16, name="hid", align_bytes=64)
            nc.vector.tensor_tensor(
                hid[:].rearrange("p (c t) -> p c t", t=PACK),
                prod[:, :, cols].rearrange("p t c -> p c t"),
                inv[b][:].rearrange("p t c -> p c t"),
                ALU.mult,
            )
            hid_codes = ring.tile([P, P], U32, name="hid_codes", align_bytes=64)
            hid_bytes = ring.tile([P, P], U8, name="hid_bytes", align_bytes=64)
            nc.vector.quantize_mx(out=hid_codes[:].bitcast(FP8X4), scales=hid_bytes[:], in_=hid[:])
            coil = acc[b % 2][:, :N].rearrange("p (a j) -> p a j", j=P)
            for a in range(N // P):
                nc.tensor.matmul_mx(
                    out=coil[:, a, :],
                    lhsT=w3_sb[:, 2 * a * P : 2 * (a + 1) * P].bitcast(FP4X4),
                    lhsT_scale=w3_plane[:, a * P : (a + 1) * P],
                    rhs=hid_codes[:].bitcast(FP8X4),
                    rhs_scale=hid_bytes[:],
                    start=True,
                    stop=True,
                )
            res = keep.tile([P, N // P, P], F32, name="res%d" % b)
            nc.scalar.copy(res[:], coil)
            nc.sync.dma_start(out.rearrange("(a p) j -> p a j", p=P)[:, :, cols], res[:])

        magnetise(0)
        field(0)
        field(1)
        numerator(0, 0, S)
        field(2)
        numerator(1, 0, S)
        inv = [psum.tile([P, PACK, P], F32, name="inv%d" % b, tag="bank%d" % b) for b in range(BLOCKS)]
        inverse_of_tile(0)
        field(3)
        numerator(2, 0, S)
        for half in range(2):
            numerator(3, half * HALF, (half + 1) * HALF)
        inverse_of_tile(1)
        prod = keep.tile([P, PACK, S], F32, tag="both")
        for b in range(BLOCKS):
            inverse_of_block(b)
        for t in range(PACK):
            product(t)
        for b in range(BLOCKS):
            coils(b)
